import numpy as np, ml_dtypes
CORES = [9,13,81,85,89,93,97,101,113,117,121,125]
N = 12
R, T = 4096, 128
CAPP = 32
def entries(a): return a.T.reshape(-1)
def pack(v, P): return np.ascontiguousarray(np.asarray(v, np.int32).reshape(-1, P).T)
def lists(rng, how):
    Q = rng.permutation(N * R)[:N * T]
    if how == "hotrank": Q = R * int(rng.integers(N)) + rng.permutation(R)[:N * T]
    if how == "own": Q = np.concatenate([R * r + rng.permutation(R)[:T] for r in range(N)])
    if how == "sorted": Q = np.sort(Q)
    if how == "edge":
        ends = np.concatenate([R * np.arange(N), R * np.arange(N) + R - 1]); rest = np.setdiff1d(rng.permutation(N * R), ends, assume_unique=True)
        Q = rng.permutation(np.concatenate([ends, rng.permutation(rest)[:N * T - 2 * N]]))
    if how in ("uniform", "full", "sorted", "edge"):
        O = np.stack([rng.permutation(np.repeat(rng.permutation(N)[:T // CAPP], CAPP)) if how == "full" else rng.permutation(np.repeat(np.arange(N), CAPP))[:T] for r in range(N)]).reshape(-1); Q = np.zeros(N * T, np.int64)
        for d in range(N):
            m = np.nonzero(O == d)[0]; w = rng.permutation(R)[:len(m)]
            if how == "edge" and len(m) >= 2: w[:2] = [0, R - 1]; w[2:] = 1 + rng.permutation(R - 2)[:len(m) - 2]
            Q[m] = R * d + w
        if how == "sorted": Q = np.sort(Q.reshape(N, T), axis=1).reshape(-1)
    return {"pos": np.stack([pack(q, 16) for q in Q.reshape(N, T)])}
def setup_inputs(rng):
    return dict({"tab": rng.standard_normal((N, 128, R), dtype=np.float32).astype(ml_dtypes.bfloat16), "new": rng.standard_normal((N, 128, T), dtype=np.float32).astype(ml_dtypes.bfloat16)}, **lists(rng, "uniform"))
def setup_inputs_edge(rng):
    d = setup_inputs(rng); d.update(lists(rng, "edge"))
    for k in ("tab", "new"): d[k] = (d[k].astype(np.float32) * 1048576.0).astype(d[k].dtype)
    return d
def setup_inputs_full(rng):
    d = setup_inputs(rng); d.update(lists(rng, "full"))
    for k in ("tab", "new"): d[k] = (d[k].astype(np.float32) * (1 / 1024.0)).astype(d[k].dtype)
    return d
def setup_inputs_sorted(rng):
    d = setup_inputs(rng); d.update(lists(rng, "sorted"))
    return d
def check_inputs(x):
    bad = []
    if x["pos"].min() < 0 or x["pos"].max() >= N * R: bad.append("pos out of range")
    if len(np.unique(x["pos"])) != x["pos"].size: bad.append("a place is named twice")
    if max(int(np.bincount(entries(a) // R, minlength=N).max()) for a in x["pos"]) > CAPP: bad.append("more than CAPP entries of a list point into one rank's part")
    return bad
def reference(tab, new, pos):
    A = np.concatenate(list(tab), axis=1)
    for r in range(N): A[:, entries(pos[r])] = new[r]
    return {"y": np.stack([A[:, R * r:R * r + R] for r in range(N)])}

@@ -1,0 +1,273 @@
+from concourse.bass import DstId, RemoteDMATransfer
+from concourse.mybir import AluOpType, AxisListType, ActivationFunctionType
+
+CAP = 32
+STR = 48
+MSG = 36
+LSTR = 40
+COLS = 4096
+WIN = 5760
+H1 = 2048
+
+SCRATCH = {
+    "posP": ("sbuf", [128, 1], "int32"),
+    "ti": ("sbuf", [128, 3], "int32"),
+    "tf": ("sbuf", [128, 3], "float32"),
+    "ip": ("sbuf", [128, 1], "int32"),
+    "ii": ("sbuf", [128, 3], "int32"),
+    "cf": ("sbuf", [128, 4], "float32"),
+    "pf": ("sbuf", [128, 1], "float32"),
+    "icol": ("sbuf", [128, 128], "float32"),
+    "destc": ("sbuf", [128, 16], "float32"),
+    "x48": ("sbuf", [128, 16], "float32"),
+    "constK": ("sbuf", [128, 256], "bfloat16"),
+    "cst4": ("sbuf", [128, 4], "float32"),
+    "mx": ("sbuf", [128, 128], "bfloat16"),
+    "my": ("sbuf", [128, 128], "bfloat16"),
+    "mtri": ("sbuf", [128, 128], "bfloat16"),
+    "a2": ("sbuf", [128, 128], "bfloat16"),
+    "maskc": ("sbuf", [128, 8], "bfloat16"),
+    "ctile": ("sbuf", [128, 64], "float32"),
+    "dd": ("sbuf", [128, 16], "bfloat16"),
+    "dx": ("sbuf", [128, 16], "float32"),
+    "junk": ("sbuf", [128, 16], "float32"),
+    "sc": ("sbuf", [128, 4], "float32"),
+    "bd": ("sbuf", [128, 32], "bfloat16"),
+    "aall": ("sbuf", [128, 256], "bfloat16"),
+    "r1": ("sbuf", [128, 8], "bfloat16"),
+    "r2": ("sbuf", [128, 8], "bfloat16"),
+    "newx": ("sbuf", [128, 192], "bfloat16"),
+    "soff": ("sbuf", [128, 12], "uint16"),
+    "send": ("sbuf", [128, 16 * STR], "bfloat16"),
+    "hbuf": ("sbuf", [128, 2 * STR + MSG], "bfloat16"),
+    "land": ("sbuf", [128, 12, LSTR], "bfloat16"),
+    "tmp": ("sbuf", [128, 12, 2], "float32"),
+    "roff": ("sbuf", [128, 24], "uint16"),
+    "flat": ("sbuf", [128, 12 * CAP], "bfloat16"),
+    "win": ("sbuf", [128, WIN], "bfloat16"),
+    "pc": ("psum", [128, 512], "float32"),
+    "po": ("psum", [128, 512], "float32"),
+    "pt": ("psum", [128, 512], "float32"),
+}
+SEMAPHORES = ["cv", "cs", "cp", "cg", "s_pos", "s_new", "s_tab1", "s_tab2", "s_y", "s_go", "s_h", "s_dir", "s_cross", "loc"]
+
+
+def _engines(mask):
+    return [e for e in range(16) if (mask >> e) & 1]
+
+
+def _mk(es):
+    return sum(1 << e for e in es)
+
+
+def _pow2(n):
+    p = 1
+    while p * 2 <= n:
+        p *= 2
+    return p
+
+
+def _plan(cores, topo):
+    classes = []
+    for r, c in enumerate(cores):
+        for cl in classes:
+            a, b = topo.chip(cores[cl[0]]), topo.chip(c)
+            if a == b or topo.same_plane(a, b):
+                cl.append(r)
+                break
+        else:
+            classes.append([r])
+    order = [r for cl in classes for r in cl]
+    xpos = {r: x for x, r in enumerate(order)}
+    direct, relay, helper = {}, {}, {}
+    for r, c in enumerate(cores):
+        direct[r] = [d for d in order if d != r and topo.may_write(c, cores[d])]
+        far = [d for d in order if d != r and not topo.may_write(c, cores[d])]
+        hs = [h for h in range(128) if topo.chip(h) == topo.chip(c) and h not in cores and topo.die(h) == topo.die(c)
+              and all(topo.may_write(h, cores[d]) for d in far)]
+        relay[r] = []
+        if far:
+            per = (len(far) + len(hs) - 1) // len(hs)
+            for i, h in enumerate(hs):
+                part = far[i * per:(i + 1) * per]
+                if part:
+                    relay[r].append((h, part))
+                    helper[h] = (r, part)
+    return classes, order, xpos, direct, relay, helper
+
+
+def _xfer(T, topo, dst_core, es, sem, src, dst):
+    rid, pid, _ = topo.addr(dst_core)
+    return RemoteDMATransfer(dst_ids=[DstId(rid=rid, pnc=pid)], dma_engine_mask=_mk(es), remote_sem=sem, src=src, dst=dst)
+
+
+def rank_program(g, core, T, topo):
+    cores = list(T.cores)
+    classes, order, xpos, direct, relay, helper = _plan(cores, topo)
+    rank = T.rank_of(core)
+    HENG = 4
+
+    if rank is None:
+        if core not in helper:
+            return
+        src, part = helper[core]
+        g.wait_ge(T.sem.s_h, HENG)
+        trs, tot = [], 0
+        for q, d in enumerate(part):
+            es = _engines(topo.mask(core, cores[d]))
+            per = _pow2(len(es) // len(part))
+            trs.append(_xfer(T, topo, cores[d], es[q * per:(q + 1) * per], T.sem.s_cross,
+                             T.hbuf[:, STR * q:STR * q + MSG], T.land[:, xpos[src], 0:MSG]))
+            tot += per
+        g.remote_dma_fused(trs, local_sem=T.sem.loc)
+        g.wait_ge(T.sem.loc, tot)
+        return
+
+    Op, Act = AluOpType, ActivationFunctionType
+    V, S, PE, Y = g.vector, g.scalar, g.tensor, g.sync
+    eng = {"v": V, "s": S, "p": PE, "g": g, "y": Y}
+    sname = {"v": "cv", "s": "cs", "p": "cp", "g": "cg"}
+    cnt = {"v": 0, "s": 0, "p": 0, "g": 0}
+    seen = {k: {} for k in eng}
+
+    def pre(q, *deps):
+        deps = list(deps)
+        if q in cnt:
+            deps.append((sname[q], cnt[q]))
+        for name, val in deps:
+            if seen[q].get(name, 0) < val:
+                eng[q].wait_ge(T.sem[name], val)
+                seen[q][name] = val
+
+    def op(q, ins):
+        cnt[q] += 1
+        ins.then_inc(T.sem[sname[q]], 1)
+        return (sname[q], cnt[q])
+
+    xs = xpos[rank]
+    mine = [cl for cl in classes if rank in cl][0]
+    x0, x1 = xpos[mine[0]], xpos[mine[-1]] + 1
+    far = [d for d in order if d not in mine]
+
+    Y.dma_start(T.posP[:], T.pos[:]).then_inc(T.sem.s_pos, 16)
+    Y.dma_start(T.newx[:, 0:128], T.new[:]).then_inc(T.sem.s_new, 16)
+    Y.dma_start(T.win[:, 0:H1], T.tab[:, 0:H1]).then_inc(T.sem.s_tab1, 16)
+
+    pre("g"); d_ip = op("g", g.iota(T.ip[:], [[0, 1]], 0, 1))
+    pre("g"); d_pf = op("g", g.iota(T.pf[:], [[0, 1]], 0, 1, allow_small_or_imprecise_dtypes=True))
+    pre("g"); d_icol = op("g", g.iota(T.icol[:], [[1, 128]], 0, 0, allow_small_or_imprecise_dtypes=True))
+    pre("g"); d_constK = op("g", g.iota(T.constK[:], [[16, 2], [0, 8], [1, 16]], 128, 0, allow_small_or_imprecise_dtypes=True))
+    pre("g"); d_cst4 = op("g", g.iota(T.cst4[:], [[1, 2], [2, 2]], CAP, 0, allow_small_or_imprecise_dtypes=True))
+    runs, a = [], 0
+    for x in range(1, len(order) + 1):
+        if x == len(order) or order[x] != order[x - 1] + 1:
+            runs.append((a, x)); a = x
+    for a, b in runs:
+        pre("g"); op("g", g.iota(T.destc[:, a:b], [[1, b - a]], order[a], 0, allow_small_or_imprecise_dtypes=True))
+    pre("g"); op("g", g.iota(T.destc[:, len(order):16], [[0, 16 - len(order)]], -1, 0, allow_small_or_imprecise_dtypes=True))
+    pre("g"); d_dest = op("g", g.iota(T.x48[:], [[STR, 16]], 0, 0, allow_small_or_imprecise_dtypes=True))
+
+    pre("v"); op("v", V.memset(T.send[:], 0.0))
+    pre("v", d_ip); op("v", V.tensor_scalar(T.ii[:, 0:1], T.ip[:], 3, None, Op.logical_shift_right))
+    pre("v"); op("v", V.tensor_scalar(T.ii[:, 1:2], T.ip[:], 7, None, Op.bitwise_and))
+    pre("v"); op("v", V.tensor_scalar(T.ii[:, 2:3], T.ip[:], 15, None, Op.bitwise_and))
+    pre("v"); op("v", V.tensor_scalar(T.cf[:, 0:1], T.ii[:, 0:1], 128.0, None, Op.add))
+    pre("v"); op("v", V.tensor_copy(T.cf[:, 1:2], T.ii[:, 1:2]))
+    pre("v"); op("v", V.tensor_scalar(T.cf[:, 2:3], T.ii[:, 2:3], float(STR), None, Op.mult))
+    pre("v"); op("v", V.tensor_scalar(T.cf[:, 3:4], T.ii[:, 2:3], -64.0, None, Op.add))
+    pre("v", d_icol); op("v", V.tensor_scalar(T.mx[:], T.icol[:], T.pf[:, 0:1], None, Op.is_gt))
+    pre("v"); op("v", V.tensor_scalar(T.my[:], T.icol[:], T.pf[:, 0:1], 128.0, Op.is_equal, Op.mult))
+    pre("v"); d_mtri = op("v", V.tensor_tensor(T.mtri[:], T.mx[:], T.my[:], Op.add))
+    pre("v"); op("v", V.tensor_scalar(T.maskc[:], T.icol[:, 0:8], T.cf[:, 1:2], None, Op.is_equal))
+    pre("v"); op("v", V.tensor_scalar(T.ctile[:], T.icol[:, 0:64], 0.0, T.cf[:, 3:4], Op.mult, Op.add))
+    for h in range(2):
+        pre("v"); op("v", V.memset(T.ctile[:, 32 * h:32 * h + 16], float(COLS + 64 * (2 * xs + h) - 8192)))
+    pre("v", d_constK); op("v", V.tensor_scalar(T.a2[:], T.constK[:, 0:128], T.cf[:, 0:1], None, Op.is_equal))
+    pre("v", d_cst4); d_vset = op("v", V.tensor_scalar(T.soff[:, 8:12], T.cst4[:], T.cf[:, 2:3], None, Op.add))
+
+    pre("v", ("s_pos", 16)); op("v", V.tensor_scalar(T.ti[:, 0:1], T.posP[:], 12, None, Op.logical_shift_right))
+    pre("v"); op("v", V.tensor_copy(T.tf[:, 0:1], T.ti[:, 0:1]))
+    pre("v", d_dest); d_dd = op("v", V.tensor_scalar(T.dd[:], T.destc[:], T.tf[:, 0:1], None, Op.is_equal))
+    pre("p", d_dd); d_pc = op("p", PE.matmul(T.pc[:, 0:16], T.mtri[:], T.dd[:], True, True))
+    pre("v"); op("v", V.tensor_scalar(T.ti[:, 1:2], T.posP[:], 4032, None, Op.bitwise_and))
+    pre("v"); op("v", V.tensor_scalar(T.ti[:, 2:3], T.posP[:], 63, None, Op.bitwise_and))
+    pre("v"); d_tf = op("v", V.tensor_copy(T.tf[:, 1:3], T.ti[:, 1:3]))
+    pre("v"); d_dx = op("v", V.tensor_tensor(T.dx[:], T.dd[:], T.x48[:], Op.mult))
+    pre("s", d_tf); op("s", S.activation(T.sc[:, 0:1], T.tf[:, 1:2], Act.Identity, bias=-8192.0))
+    pre("s"); op("s", S.activation(T.sc[:, 1:2], T.tf[:, 2:3], Act.Identity, bias=-128.0))
+    pre("s"); op("s", S.activation(T.bd[:, 0:16], T.dd[:], Act.Identity, scale=T.sc[:, 0:1]))
+    pre("s"); d_bd = op("s", S.activation(T.bd[:, 16:32], T.dd[:], Act.Identity, scale=T.sc[:, 1:2]))
+    pre("s", d_dx); op("s", S.activation(T.junk[:], T.dx[:], Act.Identity, accum_out=T.sc[:, 2:3]))
+    pre("s"); d_r1 = op("s", S.activation(T.r1[:], T.maskc[:], Act.Identity, scale=T.sc[:, 2:3]))
+    pre("p", d_r1); op("p", PE.matmul(T.po[:, 0:8], T.a2[:], T.r1[:], True, False))
+    pre("v", d_pc); d_kb = op("v", V.tensor_reduce(T.sc[:, 3:4], T.pc[:, 0:16], AxisListType.X, Op.max))
+    pre("s", d_kb); d_r2 = op("s", S.activation(T.r2[:], T.maskc[:], Act.Identity, scale=T.sc[:, 3:4]))
+    pre("p", d_r2); d_po = op("p", PE.matmul(T.po[:, 0:8], T.a2[:], T.r2[:], False, True))
+    pre("v"); d_aall = op("v", V.tensor_scalar(T.aall[:], T.constK[:], T.sc[:, 3:4], None, Op.is_equal))
+    pre("p", d_aall, d_bd); op("p", PE.matmul(T.pt[:, 0:32], T.aall[:, 0:128], T.bd[:], True, True))
+    pre("p"); d_pt = op("p", PE.matmul(T.pt[:, 32:64], T.aall[:, 128:256], T.bd[:], True, True))
+    pre("v", d_po); op("v", V.tensor_scalar(T.soff[:, 0:8], T.po[:, 0:8], -128.0, None, Op.add))
+    pre("v", d_pt); op("v", V.tensor_tensor(T.newx[:, 128:192], T.pt[:, 0:64], T.ctile[:], Op.min))
+    pre("v", ("s_new", 16))
+    d_send = op("v", V.tensor_copy(T.send[:, 0:16 * STR].indirect(T.soff[:, 0:12]), T.newx[:, 0:192]))
+
+    pre("g", d_send)
+    loc = 0
+    off_chip = [d for d in direct[rank] if topo.chip(cores[d]) != topo.chip(core)]
+    on_chip = [d for d in direct[rank] if topo.chip(cores[d]) == topo.chip(core)]
+    e_off = _engines(topo.mask(core, cores[off_chip[0]])) if off_chip else []
+    if relay[rank]:
+        e_all = _engines(topo.mask(core, relay[rank][0][0]))
+        e_on = [e for e in e_all if e not in e_off] or e_all
+        trs = []
+        for i, (h, part) in enumerate(relay[rank]):
+            a = STR * xpos[part[0]]
+            trs.append(_xfer(T, topo, h, e_on[i * HENG:(i + 1) * HENG], T.sem.s_h,
+                             T.send[:, a:a + 2 * STR + MSG], T.hbuf[:]))
+            loc += HENG
+        g.remote_dma_fused(trs, local_sem=T.sem.loc)
+    trs, n_dir = [], 0
+    per = _pow2(len(e_off) // len(off_chip)) if off_chip else 0
+    for i, d in enumerate(off_chip):
+        trs.append(_xfer(T, topo, cores[d], e_off[i * per:(i + 1) * per], T.sem.s_dir,
+                         T.send[:, STR * xpos[d]:STR * xpos[d] + MSG], T.land[:, xs, 0:MSG]))
+        loc += per
+    for d in on_chip:
+        es = [e for e in _engines(topo.mask(core, cores[d])) if e not in e_off]
+        es = es[:_pow2(len(es) // len(on_chip))]
+        trs.append(_xfer(T, topo, cores[d], es, T.sem.s_dir,
+                         T.send[:, STR * xpos[d]:STR * xpos[d] + MSG], T.land[:, xs, 0:MSG]))
+        loc += len(es)
+    g.remote_dma_fused(trs, local_sem=T.sem.loc)
+    g.sem_inc(T.sem.s_go, 1)
+    n_dir = loc - HENG * len(relay[rank])
+    n_cross = 0
+    for d in far:
+        for h, part in relay[d]:
+            if rank in part:
+                n_cross += _pow2(len(_engines(topo.mask(h, core))) // len(part))
+
+    pre("y", ("s_go", 1))
+    Y.dma_start(T.win[:, H1:COLS], T.tab[:, H1:COLS]).then_inc(T.sem.s_tab2, 16)
+
+    pre("v"); d_own = op("v", V.tensor_copy(T.land[:, xs, 0:MSG], T.send[:, STR * xs:STR * xs + MSG]))
+
+    def batch(a, b, *deps):
+        pre("s", *deps)
+        d_flat = op("s", S.activation(T.flat[:, CAP * a:CAP * b], T.land[:, a:b, 0:CAP], Act.Copy))
+        pre("v", *deps)
+        op("v", V.tensor_tensor(T.tmp[:, a:b, :], T.land[:, a:b, CAP:CAP + 2], T.land[:, a:b, CAP + 2:CAP + 4], Op.add))
+        pre("v"); op("v", V.tensor_scalar(T.roff[:, 2 * a:2 * b], T.tmp[:, a:b, :], 8320.0, None, Op.add))
+        pre("v", d_flat)
+        return op("v", V.tensor_copy(T.win[:, 0:WIN].indirect(T.roff[:, 2 * a:2 * b]), T.flat[:, CAP * a:CAP * b]))
+
+    d_last = batch(x0, x1, d_own, ("s_dir", n_dir), ("s_tab1", 16), ("s_tab2", 16))
+    if far:
+        d_last = batch(xpos[far[0]], xpos[far[-1]] + 1, ("s_cross", n_cross))
+
+    pre("y", d_last)
+    Y.dma_start(T.y[:], T.win[:, 0:COLS]).then_inc(T.sem.s_y, 16)
+    Y.wait_ge(T.sem.s_y, 16)
+
+    g.wait_ge(T.sem.loc, loc)
+    pre("g", ("cv", cnt["v"]), ("cs", cnt["s"]), ("cp", cnt["p"]))

@@ -8,6 +8,7 @@ LSTR = 40
 COLS = 4096
 WIN = 5760
 H1 = 2048
+HENG = 4
 
 SCRATCH = {
     "posP": ("sbuf", [128, 1], "int32"),
@@ -17,9 +18,8 @@ SCRATCH = {
     "ii": ("sbuf", [128, 3], "int32"),
     "cf": ("sbuf", [128, 4], "float32"),
     "pf": ("sbuf", [128, 1], "float32"),
-    "icol": ("sbuf", [128, 128], "float32"),
+    "icol": ("sbuf", [128, 128], "bfloat16"),
     "destc": ("sbuf", [128, 16], "float32"),
-    "x48": ("sbuf", [128, 16], "float32"),
     "constK": ("sbuf", [128, 256], "bfloat16"),
     "cst4": ("sbuf", [128, 4], "float32"),
     "mx": ("sbuf", [128, 128], "bfloat16"),
@@ -27,29 +27,27 @@ SCRATCH = {
     "mtri": ("sbuf", [128, 128], "bfloat16"),
     "a2": ("sbuf", [128, 128], "bfloat16"),
     "maskc": ("sbuf", [128, 8], "bfloat16"),
-    "ctile": ("sbuf", [128, 64], "float32"),
+    "ctile": ("sbuf", [128, 80], "float32"),
     "dd": ("sbuf", [128, 16], "bfloat16"),
-    "dx": ("sbuf", [128, 16], "float32"),
-    "junk": ("sbuf", [128, 16], "float32"),
     "sc": ("sbuf", [128, 4], "float32"),
     "bd": ("sbuf", [128, 32], "bfloat16"),
     "aall": ("sbuf", [128, 256], "bfloat16"),
     "r1": ("sbuf", [128, 8], "bfloat16"),
     "r2": ("sbuf", [128, 8], "bfloat16"),
-    "newx": ("sbuf", [128, 192], "bfloat16"),
+    "newx": ("sbuf", [128, 208], "bfloat16"),
+    "tmpo": ("sbuf", [128, 8], "float32"),
     "soff": ("sbuf", [128, 12], "uint16"),
     "send": ("sbuf", [128, 16 * STR], "bfloat16"),
-    "hbuf": ("sbuf", [128, 2 * STR + MSG], "bfloat16"),
     "land": ("sbuf", [128, 12, LSTR], "bfloat16"),
     "tmp": ("sbuf", [128, 12, 2], "float32"),
     "roff": ("sbuf", [128, 24], "uint16"),
     "flat": ("sbuf", [128, 12 * CAP], "bfloat16"),
     "win": ("sbuf", [128, WIN], "bfloat16"),
     "pc": ("psum", [128, 512], "float32"),
-    "po": ("psum", [128, 512], "float32"),
     "pt": ("psum", [128, 512], "float32"),
 }
-SEMAPHORES = ["cv", "cs", "cp", "cg", "s_pos", "s_new", "s_tab1", "s_tab2", "s_y", "s_go", "s_h", "s_dir", "s_cross", "loc"]
+SEMAPHORES = ["cv", "cs", "cp", "cg", "s_pos", "s_new", "s_tab1", "s_tab2", "s_y", "s_go", "s_hn", "s_h", "s_z", "s_dir",
+              "s_cross", "loc"]
 
 
 def _engines(mask):
@@ -81,19 +79,24 @@ def _plan(cores, topo):
     xpos = {r: x for x, r in enumerate(order)}
     direct, relay, helper = {}, {}, {}
     for r, c in enumerate(cores):
-        direct[r] = [d for d in order if d != r and topo.may_write(c, cores[d])]
-        far = [d for d in order if d != r and not topo.may_write(c, cores[d])]
+        direct[r] = [d for d in range(len(cores)) if d != r and topo.may_write(c, cores[d])]
+        far = [d for d in range(len(cores)) if d != r and not topo.may_write(c, cores[d])]
+        relay[r] = []
+        if not far:
+            continue
         hs = [h for h in range(128) if topo.chip(h) == topo.chip(c) and h not in cores and topo.die(h) == topo.die(c)
               and all(topo.may_write(h, cores[d]) for d in far)]
-        relay[r] = []
-        if far:
-            per = (len(far) + len(hs) - 1) // len(hs)
-            for i, h in enumerate(hs):
-                part = far[i * per:(i + 1) * per]
-                if part:
-                    relay[r].append((h, part))
-                    helper[h] = (r, part)
+        per = (len(far) + len(hs) - 1) // len(hs)
+        for i, h in enumerate(hs):
+            part = far[i * per:(i + 1) * per]
+            if part:
+                relay[r].append((h, part))
+                helper[h] = (r, part)
     return classes, order, xpos, direct, relay, helper
+
+
+def _hop2_per(topo, h, part, cores):
+    return _pow2(len(_engines(topo.mask(h, cores[part[0]]))) // len(part))
 
 
 def _xfer(T, topo, dst_core, es, sem, src, dst):
@@ -105,22 +108,7 @@ def rank_program(g, core, T, topo):
     cores = list(T.cores)
     classes, order, xpos, direct, relay, helper = _plan(cores, topo)
     rank = T.rank_of(core)
-    HENG = 4
-
-    if rank is None:
-        if core not in helper:
-            return
-        src, part = helper[core]
-        g.wait_ge(T.sem.s_h, HENG)
-        trs, tot = [], 0
-        for q, d in enumerate(part):
-            es = _engines(topo.mask(core, cores[d]))
-            per = _pow2(len(es) // len(part))
-            trs.append(_xfer(T, topo, cores[d], es[q * per:(q + 1) * per], T.sem.s_cross,
-                             T.hbuf[:, STR * q:STR * q + MSG], T.land[:, xpos[src], 0:MSG]))
-            tot += per
-        g.remote_dma_fused(trs, local_sem=T.sem.loc)
-        g.wait_ge(T.sem.loc, tot)
+    if rank is None and core not in helper:
         return
 
     Op, Act = AluOpType, ActivationFunctionType
@@ -129,6 +117,7 @@ def rank_program(g, core, T, topo):
     sname = {"v": "cv", "s": "cs", "p": "cp", "g": "cg"}
     cnt = {"v": 0, "s": 0, "p": 0, "g": 0}
     seen = {k: {} for k in eng}
+    USED = len(cores) * STR
 
     def pre(q, *deps):
         deps = list(deps)
@@ -144,126 +133,157 @@ def rank_program(g, core, T, topo):
         ins.then_inc(T.sem[sname[q]], 1)
         return (sname[q], cnt[q])
 
+    def place_offsets(d_ip, d_cst4):
+        pre("v", d_ip); op("v", V.tensor_scalar(T.ii[:, 2:3], T.ip[:], 15, None, Op.bitwise_and))
+        pre("v"); op("v", V.tensor_scalar(T.cf[:, 2:3], T.ii[:, 2:3], float(STR), None, Op.mult))
+        pre("v", d_cst4); op("v", V.tensor_scalar(T.soff[:, 8:12], T.cst4[:], T.cf[:, 2:3], None, Op.add))
+
+    def fill_buckets(*deps):
+        pre("v", *deps); op("v", V.tensor_tensor(T.tmpo[:], T.newx[:, 192:200], T.newx[:, 200:208], Op.add))
+        pre("v"); op("v", V.tensor_scalar(T.soff[:, 0:8], T.tmpo[:], -128.0, None, Op.add))
+        pre("v")
+        return op("v", V.tensor_copy(T.send[:, 0:16 * STR].indirect(T.soff[:, 0:12]), T.newx[:, 0:192]))
+
+    if rank is None:
+        src, part = helper[core]
+        hs = [h for h, _ in relay[src]]
+        i, n = hs.index(core), len(hs)
+        e_far = _engines(topo.mask(core, cores[part[0]]))
+        pre("v"); d_zero = op("v", V.memset(T.send[:, 0:USED], 0.0))
+        pre("g"); d_ip = op("g", g.iota(T.ip[:], [[0, 1]], 0, 1))
+        pre("g"); d_cst4 = op("g", g.iota(T.cst4[:], [[1, 2], [2, 2]], CAP, 0, allow_small_or_imprecise_dtypes=True))
+        pre("g", d_zero)
+        rid, pid, _ = topo.addr(cores[src])
+        a, b = USED * i // n, USED * (i + 1) // n
+        g.remote_dma(T.send[:, a:b], T.send[:, a:b], T.sem.s_z, T.sem.loc, pid, rid, _mk(e_far))
+        place_offsets(d_ip, d_cst4)
+        d_send = fill_buckets(("s_hn", HENG), ("s_h", HENG), ("loc", len(e_far)))
+        pre("g", d_send)
+        per = _hop2_per(topo, core, part, cores)
+        trs = []
+        for q, d in enumerate(part):
+            trs.append(_xfer(T, topo, cores[d], e_far[q * per:(q + 1) * per], T.sem.s_cross,
+                             T.send[:, STR * d:STR * d + MSG], T.land[:, xpos[src], 0:MSG]))
+        g.remote_dma_fused(trs, local_sem=T.sem.loc)
+        g.wait_ge(T.sem.loc, len(e_far) + per * len(trs))
+        return
+
     xs = xpos[rank]
     mine = [cl for cl in classes if rank in cl][0]
     x0, x1 = xpos[mine[0]], xpos[mine[-1]] + 1
     far = [d for d in order if d not in mine]
+    off_chip = [d for d in direct[rank] if topo.chip(cores[d]) != topo.chip(core)]
+    on_chip = [d for d in direct[rank] if topo.chip(cores[d]) == topo.chip(core)]
+    e_off = _engines(topo.mask(core, cores[off_chip[0]])) if off_chip else []
+    loc = 0
+
+    def to_helpers(a, b, sem):
+        trs = []
+        for i, (h, _) in enumerate(relay[rank]):
+            e_all = _engines(topo.mask(core, h))
+            e_on = [e for e in e_all if e not in e_off] or e_all
+            trs.append(_xfer(T, topo, h, e_on[i * HENG:(i + 1) * HENG], sem, T.newx[:, a:b], T.newx[:, a:b]))
+        if trs:
+            g.remote_dma_fused(trs, local_sem=T.sem.loc)
+        return HENG * len(trs)
 
     Y.dma_start(T.posP[:], T.pos[:]).then_inc(T.sem.s_pos, 16)
     Y.dma_start(T.newx[:, 0:128], T.new[:]).then_inc(T.sem.s_new, 16)
     Y.dma_start(T.win[:, 0:H1], T.tab[:, 0:H1]).then_inc(T.sem.s_tab1, 16)
 
     pre("g"); d_ip = op("g", g.iota(T.ip[:], [[0, 1]], 0, 1))
-    pre("g"); d_pf = op("g", g.iota(T.pf[:], [[0, 1]], 0, 1, allow_small_or_imprecise_dtypes=True))
     pre("g"); d_icol = op("g", g.iota(T.icol[:], [[1, 128]], 0, 0, allow_small_or_imprecise_dtypes=True))
+    pre("g"); d_dest = op("g", g.iota(T.destc[:], [[1, 16]], 0, 0, allow_small_or_imprecise_dtypes=True))
     pre("g"); d_constK = op("g", g.iota(T.constK[:], [[16, 2], [0, 8], [1, 16]], 128, 0, allow_small_or_imprecise_dtypes=True))
     pre("g"); d_cst4 = op("g", g.iota(T.cst4[:], [[1, 2], [2, 2]], CAP, 0, allow_small_or_imprecise_dtypes=True))
-    runs, a = [], 0
-    for x in range(1, len(order) + 1):
-        if x == len(order) or order[x] != order[x - 1] + 1:
-            runs.append((a, x)); a = x
-    for a, b in runs:
-        pre("g"); op("g", g.iota(T.destc[:, a:b], [[1, b - a]], order[a], 0, allow_small_or_imprecise_dtypes=True))
-    pre("g"); op("g", g.iota(T.destc[:, len(order):16], [[0, 16 - len(order)]], -1, 0, allow_small_or_imprecise_dtypes=True))
-    pre("g"); d_dest = op("g", g.iota(T.x48[:], [[STR, 16]], 0, 0, allow_small_or_imprecise_dtypes=True))
+    pre("g", ("s_new", 16))
+    loc += to_helpers(0, 128, T.sem.s_hn)
 
-    pre("v"); op("v", V.memset(T.send[:], 0.0))
-    pre("v", d_ip); op("v", V.tensor_scalar(T.ii[:, 0:1], T.ip[:], 3, None, Op.logical_shift_right))
+    pre("v", d_ip); op("v", V.tensor_copy(T.pf[:], T.ip[:]))
+    pre("v"); op("v", V.tensor_scalar(T.ii[:, 0:1], T.ip[:], 3, None, Op.logical_shift_right))
     pre("v"); op("v", V.tensor_scalar(T.ii[:, 1:2], T.ip[:], 7, None, Op.bitwise_and))
     pre("v"); op("v", V.tensor_scalar(T.ii[:, 2:3], T.ip[:], 15, None, Op.bitwise_and))
     pre("v"); op("v", V.tensor_scalar(T.cf[:, 0:1], T.ii[:, 0:1], 128.0, None, Op.add))
     pre("v"); op("v", V.tensor_copy(T.cf[:, 1:2], T.ii[:, 1:2]))
-    pre("v"); op("v", V.tensor_scalar(T.cf[:, 2:3], T.ii[:, 2:3], float(STR), None, Op.mult))
     pre("v"); op("v", V.tensor_scalar(T.cf[:, 3:4], T.ii[:, 2:3], -64.0, None, Op.add))
     pre("v", d_icol); op("v", V.tensor_scalar(T.mx[:], T.icol[:], T.pf[:, 0:1], None, Op.is_gt))
     pre("v"); op("v", V.tensor_scalar(T.my[:], T.icol[:], T.pf[:, 0:1], 128.0, Op.is_equal, Op.mult))
-    pre("v"); d_mtri = op("v", V.tensor_tensor(T.mtri[:], T.mx[:], T.my[:], Op.add))
+    pre("v"); op("v", V.tensor_tensor(T.mtri[:], T.mx[:], T.my[:], Op.add))
     pre("v"); op("v", V.tensor_scalar(T.maskc[:], T.icol[:, 0:8], T.cf[:, 1:2], None, Op.is_equal))
-    pre("v"); op("v", V.tensor_scalar(T.ctile[:], T.icol[:, 0:64], 0.0, T.cf[:, 3:4], Op.mult, Op.add))
+    pre("v"); op("v", V.tensor_scalar(T.ctile[:, 0:64], T.icol[:, 0:64], 0.0, T.cf[:, 3:4], Op.mult, Op.add))
     for h in range(2):
         pre("v"); op("v", V.memset(T.ctile[:, 32 * h:32 * h + 16], float(COLS + 64 * (2 * xs + h) - 8192)))
+    pre("v"); op("v", V.memset(T.ctile[:, 64:80], 10000.0))
     pre("v", d_constK); op("v", V.tensor_scalar(T.a2[:], T.constK[:, 0:128], T.cf[:, 0:1], None, Op.is_equal))
-    pre("v", d_cst4); d_vset = op("v", V.tensor_scalar(T.soff[:, 8:12], T.cst4[:], T.cf[:, 2:3], None, Op.add))
 
     pre("v", ("s_pos", 16)); op("v", V.tensor_scalar(T.ti[:, 0:1], T.posP[:], 12, None, Op.logical_shift_right))
-    pre("v"); op("v", V.tensor_copy(T.tf[:, 0:1], T.ti[:, 0:1]))
+    pre("v"); d_df = op("v", V.tensor_copy(T.tf[:, 0:1], T.ti[:, 0:1]))
     pre("v", d_dest); d_dd = op("v", V.tensor_scalar(T.dd[:], T.destc[:], T.tf[:, 0:1], None, Op.is_equal))
     pre("p", d_dd); d_pc = op("p", PE.matmul(T.pc[:, 0:16], T.mtri[:], T.dd[:], True, True))
+    pre("s", d_df); op("s", S.activation(T.sc[:, 2:3], T.tf[:, 0:1], Act.Identity, scale=float(STR)))
+    pre("s"); d_r1 = op("s", S.activation(T.r1[:], T.maskc[:], Act.Identity, scale=T.sc[:, 2:3]))
+    pre("p", d_r1); op("p", PE.matmul(T.pt[:, 64:72], T.a2[:], T.r1[:], True, True))
     pre("v"); op("v", V.tensor_scalar(T.ti[:, 1:2], T.posP[:], 4032, None, Op.bitwise_and))
     pre("v"); op("v", V.tensor_scalar(T.ti[:, 2:3], T.posP[:], 63, None, Op.bitwise_and))
     pre("v"); d_tf = op("v", V.tensor_copy(T.tf[:, 1:3], T.ti[:, 1:3]))
-    pre("v"); d_dx = op("v", V.tensor_tensor(T.dx[:], T.dd[:], T.x48[:], Op.mult))
     pre("s", d_tf); op("s", S.activation(T.sc[:, 0:1], T.tf[:, 1:2], Act.Identity, bias=-8192.0))
     pre("s"); op("s", S.activation(T.sc[:, 1:2], T.tf[:, 2:3], Act.Identity, bias=-128.0))
     pre("s"); op("s", S.activation(T.bd[:, 0:16], T.dd[:], Act.Identity, scale=T.sc[:, 0:1]))
     pre("s"); d_bd = op("s", S.activation(T.bd[:, 16:32], T.dd[:], Act.Identity, scale=T.sc[:, 1:2]))
-    pre("s", d_dx); op("s", S.activation(T.junk[:], T.dx[:], Act.Identity, accum_out=T.sc[:, 2:3]))
-    pre("s"); d_r1 = op("s", S.activation(T.r1[:], T.maskc[:], Act.Identity, scale=T.sc[:, 2:3]))
-    pre("p", d_r1); op("p", PE.matmul(T.po[:, 0:8], T.a2[:], T.r1[:], True, False))
     pre("v", d_pc); d_kb = op("v", V.tensor_reduce(T.sc[:, 3:4], T.pc[:, 0:16], AxisListType.X, Op.max))
     pre("s", d_kb); d_r2 = op("s", S.activation(T.r2[:], T.maskc[:], Act.Identity, scale=T.sc[:, 3:4]))
-    pre("p", d_r2); d_po = op("p", PE.matmul(T.po[:, 0:8], T.a2[:], T.r2[:], False, True))
     pre("v"); d_aall = op("v", V.tensor_scalar(T.aall[:], T.constK[:], T.sc[:, 3:4], None, Op.is_equal))
     pre("p", d_aall, d_bd); op("p", PE.matmul(T.pt[:, 0:32], T.aall[:, 0:128], T.bd[:], True, True))
-    pre("p"); d_pt = op("p", PE.matmul(T.pt[:, 32:64], T.aall[:, 128:256], T.bd[:], True, True))
-    pre("v", d_po); op("v", V.tensor_scalar(T.soff[:, 0:8], T.po[:, 0:8], -128.0, None, Op.add))
-    pre("v", d_pt); op("v", V.tensor_tensor(T.newx[:, 128:192], T.pt[:, 0:64], T.ctile[:], Op.min))
-    pre("v", ("s_new", 16))
-    d_send = op("v", V.tensor_copy(T.send[:, 0:16 * STR].indirect(T.soff[:, 0:12]), T.newx[:, 0:192]))
+    pre("p"); op("p", PE.matmul(T.pt[:, 32:64], T.aall[:, 128:256], T.bd[:], True, True))
+    pre("p", d_r2); d_pt = op("p", PE.matmul(T.pt[:, 72:80], T.a2[:], T.r2[:], True, True))
+    pre("v", d_pt); d_msg = op("v", V.tensor_tensor(T.newx[:, 128:208], T.pt[:, 0:80], T.ctile[:], Op.min))
 
+    pre("g", d_msg)
+    loc += to_helpers(128, 208, T.sem.s_h)
+    place_offsets(d_ip, d_cst4)
+    n_z = sum(len(_engines(topo.mask(h, cores[part[0]]))) for h, part in relay[rank])
+    if not relay[rank]:
+        pre("v"); op("v", V.memset(T.send[:, 0:USED], 0.0))
+    d_send = fill_buckets(("s_new", 16), ("s_z", n_z))
     pre("g", d_send)
-    loc = 0
-    off_chip = [d for d in direct[rank] if topo.chip(cores[d]) != topo.chip(core)]
-    on_chip = [d for d in direct[rank] if topo.chip(cores[d]) == topo.chip(core)]
-    e_off = _engines(topo.mask(core, cores[off_chip[0]])) if off_chip else []
-    if relay[rank]:
-        e_all = _engines(topo.mask(core, relay[rank][0][0]))
-        e_on = [e for e in e_all if e not in e_off] or e_all
-        trs = []
-        for i, (h, part) in enumerate(relay[rank]):
-            a = STR * xpos[part[0]]
-            trs.append(_xfer(T, topo, h, e_on[i * HENG:(i + 1) * HENG], T.sem.s_h,
-                             T.send[:, a:a + 2 * STR + MSG], T.hbuf[:]))
-            loc += HENG
-        g.remote_dma_fused(trs, local_sem=T.sem.loc)
     trs, n_dir = [], 0
     per = _pow2(len(e_off) // len(off_chip)) if off_chip else 0
     for i, d in enumerate(off_chip):
         trs.append(_xfer(T, topo, cores[d], e_off[i * per:(i + 1) * per], T.sem.s_dir,
-                         T.send[:, STR * xpos[d]:STR * xpos[d] + MSG], T.land[:, xs, 0:MSG]))
-        loc += per
+                         T.send[:, STR * d:STR * d + MSG], T.land[:, xs, 0:MSG]))
+        n_dir += per
     for d in on_chip:
         es = [e for e in _engines(topo.mask(core, cores[d])) if e not in e_off]
         es = es[:_pow2(len(es) // len(on_chip))]
         trs.append(_xfer(T, topo, cores[d], es, T.sem.s_dir,
-                         T.send[:, STR * xpos[d]:STR * xpos[d] + MSG], T.land[:, xs, 0:MSG]))
-        loc += len(es)
+                         T.send[:, STR * d:STR * d + MSG], T.land[:, xs, 0:MSG]))
+        n_dir += len(es)
     g.remote_dma_fused(trs, local_sem=T.sem.loc)
     g.sem_inc(T.sem.s_go, 1)
-    n_dir = loc - HENG * len(relay[rank])
+    loc += n_dir
     n_cross = 0
     for d in far:
         for h, part in relay[d]:
             if rank in part:
-                n_cross += _pow2(len(_engines(topo.mask(h, core))) // len(part))
+                n_cross += _hop2_per(topo, h, part, cores)
 
     pre("y", ("s_go", 1))
     Y.dma_start(T.win[:, H1:COLS], T.tab[:, H1:COLS]).then_inc(T.sem.s_tab2, 16)
 
-    pre("v"); d_own = op("v", V.tensor_copy(T.land[:, xs, 0:MSG], T.send[:, STR * xs:STR * xs + MSG]))
+    pre("v"); d_own = op("v", V.tensor_copy(T.land[:, xs, 0:MSG], T.send[:, STR * rank:STR * rank + MSG]))
 
-    def batch(a, b, *deps):
+    def batch(a, b, deps, late):
         pre("s", *deps)
         d_flat = op("s", S.activation(T.flat[:, CAP * a:CAP * b], T.land[:, a:b, 0:CAP], Act.Copy))
         pre("v", *deps)
         op("v", V.tensor_tensor(T.tmp[:, a:b, :], T.land[:, a:b, CAP:CAP + 2], T.land[:, a:b, CAP + 2:CAP + 4], Op.add))
         pre("v"); op("v", V.tensor_scalar(T.roff[:, 2 * a:2 * b], T.tmp[:, a:b, :], 8320.0, None, Op.add))
-        pre("v", d_flat)
+        pre("v", d_flat, *late)
         return op("v", V.tensor_copy(T.win[:, 0:WIN].indirect(T.roff[:, 2 * a:2 * b]), T.flat[:, CAP * a:CAP * b]))
 
-    d_last = batch(x0, x1, d_own, ("s_dir", n_dir), ("s_tab1", 16), ("s_tab2", 16))
+    d_last = batch(x0, x1, [d_own, ("s_dir", n_dir)], [("s_tab1", 16), ("s_tab2", 16)])
     if far:
-        d_last = batch(xpos[far[0]], xpos[far[-1]] + 1, ("s_cross", n_cross))
+        d_last = batch(xpos[far[0]], xpos[far[-1]] + 1, [("s_cross", n_cross)], [])
 
     pre("y", d_last)
     Y.dma_start(T.y[:], T.win[:, 0:COLS]).then_inc(T.sem.s_y, 16)

@@ -8,7 +8,6 @@ LSTR = 40
 COLS = 4096
 WIN = 5760
 H1 = 2048
-HENG = 4
 
 SCRATCH = {
     "posP": ("sbuf", [128, 1], "int32"),
@@ -46,8 +45,8 @@ SCRATCH = {
     "pc": ("psum", [128, 512], "float32"),
     "pt": ("psum", [128, 512], "float32"),
 }
-SEMAPHORES = ["cv", "cs", "cp", "cg", "s_pos", "s_new", "s_tab1", "s_tab2", "s_y", "s_go", "s_hn", "s_h", "s_z", "s_dir",
-              "s_cross", "loc"]
+SEMAPHORES = ["cv", "cs", "cp", "cg", "s_pos", "s_new", "s_tab1", "s_tab2", "s_y", "s_go", "s_c", "s_hn", "s_h", "s_z",
+              "s_dir", "s_cross", "s_late", "loc"]
 
 
 def _engines(mask):
@@ -87,16 +86,26 @@ def _plan(cores, topo):
         hs = [h for h in range(128) if topo.chip(h) == topo.chip(c) and h not in cores and topo.die(h) == topo.die(c)
               and all(topo.may_write(h, cores[d]) for d in far)]
         per = (len(far) + len(hs) - 1) // len(hs)
+        rot = [cl for cl in classes if r in cl][0].index(r)
         for i, h in enumerate(hs):
             part = far[i * per:(i + 1) * per]
             if part:
+                k = rot % len(part)
+                part = part[k:] + part[:k]
                 relay[r].append((h, part))
                 helper[h] = (r, part)
     return classes, order, xpos, direct, relay, helper
 
 
-def _hop2_per(topo, h, part, cores):
-    return _pow2(len(_engines(topo.mask(h, cores[part[0]]))) // len(part))
+def _hop2_calls(topo, h, part, cores):
+    es = _engines(topo.mask(h, cores[part[0]]))
+    calls, rest = [], list(part)
+    while rest:
+        m = min(_pow2(len(rest)), len(es))
+        per = len(es) // m
+        calls.append([(d, es[q * per:(q + 1) * per]) for q, d in enumerate(rest[:m])])
+        rest = rest[m:]
+    return calls
 
 
 def _xfer(T, topo, dst_core, es, sem, src, dst):
@@ -133,10 +142,28 @@ def rank_program(g, core, T, topo):
         ins.then_inc(T.sem[sname[q]], 1)
         return (sname[q], cnt[q])
 
-    def place_offsets(d_ip, d_cst4):
-        pre("v", d_ip); op("v", V.tensor_scalar(T.ii[:, 2:3], T.ip[:], 15, None, Op.bitwise_and))
-        pre("v"); op("v", V.tensor_scalar(T.cf[:, 2:3], T.ii[:, 2:3], float(STR), None, Op.mult))
-        pre("v", d_cst4); op("v", V.tensor_scalar(T.soff[:, 8:12], T.cst4[:], T.cf[:, 2:3], None, Op.add))
+    def arrivals(r):
+        mine = [cl for cl in classes if r in cl][0]
+        first, later = [], []
+        for s in order:
+            for h, part in relay[s]:
+                for ci, call in enumerate(_hop2_calls(topo, h, part, cores)):
+                    for d, es in call:
+                        if d == r:
+                            (first if ci == 0 else later).append((s, len(es)))
+        return mine, first, later
+
+    def lslot(r, s):
+        mine, first, later = arrivals(r)
+        return (list(mine) + [t for t, _ in first] + [t for t, _ in later]).index(s)
+
+    def hop1_engines(r):
+        out = []
+        for i, (h, _) in enumerate(relay[r]):
+            es = _engines(topo.mask(cores[r], h))
+            per = _pow2(len(es) // len(relay[r]))
+            out.append(es[len(es) - (i + 1) * per:len(es) - i * per])
+        return out
 
     def fill_buckets(*deps):
         pre("v", *deps); op("v", V.tensor_tensor(T.tmpo[:], T.newx[:, 192:200], T.newx[:, 200:208], Op.add))
@@ -148,73 +175,72 @@ def rank_program(g, core, T, topo):
         src, part = helper[core]
         hs = [h for h, _ in relay[src]]
         i, n = hs.index(core), len(hs)
+        heng = len(hop1_engines(src)[i])
         e_far = _engines(topo.mask(core, cores[part[0]]))
         pre("v"); d_zero = op("v", V.memset(T.send[:, 0:USED], 0.0))
-        pre("g"); d_ip = op("g", g.iota(T.ip[:], [[0, 1]], 0, 1))
-        pre("g"); d_cst4 = op("g", g.iota(T.cst4[:], [[1, 2], [2, 2]], CAP, 0, allow_small_or_imprecise_dtypes=True))
         pre("g", d_zero)
         rid, pid, _ = topo.addr(cores[src])
         a, b = USED * i // n, USED * (i + 1) // n
         g.remote_dma(T.send[:, a:b], T.send[:, a:b], T.sem.s_z, T.sem.loc, pid, rid, _mk(e_far))
-        place_offsets(d_ip, d_cst4)
-        d_send = fill_buckets(("s_hn", HENG), ("s_h", HENG), ("loc", len(e_far)))
+        d_send = fill_buckets(("s_c", heng), ("s_hn", heng), ("s_h", heng), ("loc", len(e_far)))
         pre("g", d_send)
-        per = _hop2_per(topo, core, part, cores)
-        trs = []
-        for q, d in enumerate(part):
-            trs.append(_xfer(T, topo, cores[d], e_far[q * per:(q + 1) * per], T.sem.s_cross,
-                             T.send[:, STR * d:STR * d + MSG], T.land[:, xpos[src], 0:MSG]))
-        g.remote_dma_fused(trs, local_sem=T.sem.loc)
-        g.wait_ge(T.sem.loc, len(e_far) + per * len(trs))
+        tot = len(e_far)
+        for ci, call in enumerate(_hop2_calls(topo, core, part, cores)):
+            sem = T.sem.s_cross if ci == 0 else T.sem.s_late
+            g.remote_dma_fused([_xfer(T, topo, cores[d], es, sem, T.send[:, STR * d:STR * d + MSG],
+                                      T.land[:, lslot(d, src), 0:MSG]) for d, es in call], local_sem=T.sem.loc)
+            tot += sum(len(es) for _, es in call)
+        g.wait_ge(T.sem.loc, tot)
         return
 
     xs = xpos[rank]
-    mine = [cl for cl in classes if rank in cl][0]
-    x0, x1 = xpos[mine[0]], xpos[mine[-1]] + 1
-    far = [d for d in order if d not in mine]
+    mine, first, later = arrivals(rank)
     off_chip = [d for d in direct[rank] if topo.chip(cores[d]) != topo.chip(core)]
     on_chip = [d for d in direct[rank] if topo.chip(cores[d]) == topo.chip(core)]
     e_off = _engines(topo.mask(core, cores[off_chip[0]])) if off_chip else []
     loc = 0
 
-    def to_helpers(a, b, sem):
-        trs = []
-        for i, (h, _) in enumerate(relay[rank]):
-            e_all = _engines(topo.mask(core, h))
-            e_on = [e for e in e_all if e not in e_off] or e_all
-            trs.append(_xfer(T, topo, h, e_on[i * HENG:(i + 1) * HENG], sem, T.newx[:, a:b], T.newx[:, a:b]))
+    def to_helpers(ap, sem):
+        trs = [_xfer(T, topo, h, es, sem, ap, ap) for (h, _), es in zip(relay[rank], hop1_engines(rank))]
         if trs:
             g.remote_dma_fused(trs, local_sem=T.sem.loc)
-        return HENG * len(trs)
+        return sum(len(es) for es in hop1_engines(rank))
 
     Y.dma_start(T.posP[:], T.pos[:]).then_inc(T.sem.s_pos, 16)
     Y.dma_start(T.newx[:, 0:128], T.new[:]).then_inc(T.sem.s_new, 16)
     Y.dma_start(T.win[:, 0:H1], T.tab[:, 0:H1]).then_inc(T.sem.s_tab1, 16)
 
     pre("g"); d_ip = op("g", g.iota(T.ip[:], [[0, 1]], 0, 1))
+    pre("g"); d_cst4 = op("g", g.iota(T.cst4[:], [[1, 2], [2, 2]], CAP, 0, allow_small_or_imprecise_dtypes=True))
     pre("g"); d_icol = op("g", g.iota(T.icol[:], [[1, 128]], 0, 0, allow_small_or_imprecise_dtypes=True))
     pre("g"); d_dest = op("g", g.iota(T.destc[:], [[1, 16]], 0, 0, allow_small_or_imprecise_dtypes=True))
+    pre("v", d_ip); op("v", V.tensor_scalar(T.ii[:, 2:3], T.ip[:], 15, None, Op.bitwise_and))
+    pre("v"); op("v", V.tensor_scalar(T.cf[:, 2:3], T.ii[:, 2:3], float(STR), None, Op.mult))
+    pre("v", d_cst4); d_soffc = op("v", V.tensor_scalar(T.soff[:, 8:12], T.cst4[:], T.cf[:, 2:3], None, Op.add))
+    pre("g", d_soffc)
+    loc += to_helpers(T.soff[:, 8:12], T.sem.s_c)
     pre("g"); d_constK = op("g", g.iota(T.constK[:], [[16, 2], [0, 8], [1, 16]], 128, 0, allow_small_or_imprecise_dtypes=True))
-    pre("g"); d_cst4 = op("g", g.iota(T.cst4[:], [[1, 2], [2, 2]], CAP, 0, allow_small_or_imprecise_dtypes=True))
     pre("g", ("s_new", 16))
-    loc += to_helpers(0, 128, T.sem.s_hn)
+    loc += to_helpers(T.newx[:, 0:128], T.sem.s_hn)
 
-    pre("v", d_ip); op("v", V.tensor_copy(T.pf[:], T.ip[:]))
+    pre("v"); op("v", V.tensor_copy(T.pf[:], T.ip[:]))
+    pre("v"); d_cf3 = op("v", V.tensor_scalar(T.cf[:, 3:4], T.ii[:, 2:3], -64.0, None, Op.add))
     pre("v"); op("v", V.tensor_scalar(T.ii[:, 0:1], T.ip[:], 3, None, Op.logical_shift_right))
     pre("v"); op("v", V.tensor_scalar(T.ii[:, 1:2], T.ip[:], 7, None, Op.bitwise_and))
-    pre("v"); op("v", V.tensor_scalar(T.ii[:, 2:3], T.ip[:], 15, None, Op.bitwise_and))
     pre("v"); op("v", V.tensor_scalar(T.cf[:, 0:1], T.ii[:, 0:1], 128.0, None, Op.add))
     pre("v"); op("v", V.tensor_copy(T.cf[:, 1:2], T.ii[:, 1:2]))
-    pre("v"); op("v", V.tensor_scalar(T.cf[:, 3:4], T.ii[:, 2:3], -64.0, None, Op.add))
     pre("v", d_icol); op("v", V.tensor_scalar(T.mx[:], T.icol[:], T.pf[:, 0:1], None, Op.is_gt))
     pre("v"); op("v", V.tensor_scalar(T.my[:], T.icol[:], T.pf[:, 0:1], 128.0, Op.is_equal, Op.mult))
     pre("v"); op("v", V.tensor_tensor(T.mtri[:], T.mx[:], T.my[:], Op.add))
     pre("v"); op("v", V.tensor_scalar(T.maskc[:], T.icol[:, 0:8], T.cf[:, 1:2], None, Op.is_equal))
-    pre("v"); op("v", V.tensor_scalar(T.ctile[:, 0:64], T.icol[:, 0:64], 0.0, T.cf[:, 3:4], Op.mult, Op.add))
-    for h in range(2):
-        pre("v"); op("v", V.memset(T.ctile[:, 32 * h:32 * h + 16], float(COLS + 64 * (2 * xs + h) - 8192)))
-    pre("v"); op("v", V.memset(T.ctile[:, 64:80], 10000.0))
     pre("v", d_constK); op("v", V.tensor_scalar(T.a2[:], T.constK[:, 0:128], T.cf[:, 0:1], None, Op.is_equal))
+
+    pre("s", d_cf3, d_icol)
+    op("s", S.activation(T.ctile[:, 0:64], T.icol[:, 0:64], Act.Identity, bias=T.cf[:, 3:4], scale=0.0))
+    for h in range(2):
+        pre("s"); op("s", S.activation(T.ctile[:, 32 * h:32 * h + 16], T.icol[:, 0:16], Act.Identity,
+                                       bias=float(COLS + 64 * (2 * xs + h) - 8192), scale=0.0))
+    pre("s"); d_ctile = op("s", S.activation(T.ctile[:, 64:80], T.icol[:, 0:16], Act.Identity, bias=10000.0, scale=0.0))
 
     pre("v", ("s_pos", 16)); op("v", V.tensor_scalar(T.ti[:, 0:1], T.posP[:], 12, None, Op.logical_shift_right))
     pre("v"); d_df = op("v", V.tensor_copy(T.tf[:, 0:1], T.ti[:, 0:1]))
@@ -236,11 +262,10 @@ def rank_program(g, core, T, topo):
     pre("p", d_aall, d_bd); op("p", PE.matmul(T.pt[:, 0:32], T.aall[:, 0:128], T.bd[:], True, True))
     pre("p"); op("p", PE.matmul(T.pt[:, 32:64], T.aall[:, 128:256], T.bd[:], True, True))
     pre("p", d_r2); d_pt = op("p", PE.matmul(T.pt[:, 72:80], T.a2[:], T.r2[:], True, True))
-    pre("v", d_pt); d_msg = op("v", V.tensor_tensor(T.newx[:, 128:208], T.pt[:, 0:80], T.ctile[:], Op.min))
+    pre("v", d_pt, d_ctile); d_msg = op("v", V.tensor_tensor(T.newx[:, 128:208], T.pt[:, 0:80], T.ctile[:], Op.min))
 
     pre("g", d_msg)
-    loc += to_helpers(128, 208, T.sem.s_h)
-    place_offsets(d_ip, d_cst4)
+    loc += to_helpers(T.newx[:, 128:208], T.sem.s_h)
     n_z = sum(len(_engines(topo.mask(h, cores[part[0]]))) for h, part in relay[rank])
     if not relay[rank]:
         pre("v"); op("v", V.memset(T.send[:, 0:USED], 0.0))
@@ -250,27 +275,23 @@ def rank_program(g, core, T, topo):
     per = _pow2(len(e_off) // len(off_chip)) if off_chip else 0
     for i, d in enumerate(off_chip):
         trs.append(_xfer(T, topo, cores[d], e_off[i * per:(i + 1) * per], T.sem.s_dir,
-                         T.send[:, STR * d:STR * d + MSG], T.land[:, xs, 0:MSG]))
+                         T.send[:, STR * d:STR * d + MSG], T.land[:, lslot(d, rank), 0:MSG]))
         n_dir += per
     for d in on_chip:
         es = [e for e in _engines(topo.mask(core, cores[d])) if e not in e_off]
         es = es[:_pow2(len(es) // len(on_chip))]
         trs.append(_xfer(T, topo, cores[d], es, T.sem.s_dir,
-                         T.send[:, STR * d:STR * d + MSG], T.land[:, xs, 0:MSG]))
+                         T.send[:, STR * d:STR * d + MSG], T.land[:, lslot(d, rank), 0:MSG]))
         n_dir += len(es)
     g.remote_dma_fused(trs, local_sem=T.sem.loc)
     g.sem_inc(T.sem.s_go, 1)
     loc += n_dir
-    n_cross = 0
-    for d in far:
-        for h, part in relay[d]:
-            if rank in part:
-                n_cross += _hop2_per(topo, h, part, cores)
 
     pre("y", ("s_go", 1))
     Y.dma_start(T.win[:, H1:COLS], T.tab[:, H1:COLS]).then_inc(T.sem.s_tab2, 16)
 
-    pre("v"); d_own = op("v", V.tensor_copy(T.land[:, xs, 0:MSG], T.send[:, STR * rank:STR * rank + MSG]))
+    pre("v")
+    d_own = op("v", V.tensor_copy(T.land[:, lslot(rank, rank), 0:MSG], T.send[:, STR * rank:STR * rank + MSG]))
 
     def batch(a, b, deps, late):
         pre("s", *deps)
@@ -281,9 +302,12 @@ def rank_program(g, core, T, topo):
         pre("v", d_flat, *late)
         return op("v", V.tensor_copy(T.win[:, 0:WIN].indirect(T.roff[:, 2 * a:2 * b]), T.flat[:, CAP * a:CAP * b]))
 
-    d_last = batch(x0, x1, [d_own, ("s_dir", n_dir)], [("s_tab1", 16), ("s_tab2", 16)])
-    if far:
-        d_last = batch(xpos[far[0]], xpos[far[-1]] + 1, [("s_cross", n_cross)], [])
+    n0, n1, n2 = len(mine), len(first), len(later)
+    d_last = batch(0, n0, [d_own, ("s_dir", n_dir)], [("s_tab1", 16), ("s_tab2", 16)])
+    if n1:
+        d_last = batch(n0, n0 + n1, [("s_cross", sum(e for _, e in first))], [])
+    if n2:
+        d_last = batch(n0 + n1, n0 + n1 + n2, [("s_late", sum(e for _, e in later))], [])
 
     pre("y", d_last)
     Y.dma_start(T.y[:], T.win[:, 0:COLS]).then_inc(T.sem.s_y, 16)

from concourse.bass import DstId, RemoteDMATransfer
from concourse.mybir import AluOpType, AxisListType, ActivationFunctionType

CAP = 32
STR = 48
MSG = 36
LSTR = 40
COLS = 4096
WIN = 5760
H1 = 2048

SCRATCH = {
    "posP": ("sbuf", [128, 1], "int32"),
    "ti": ("sbuf", [128, 3], "int32"),
    "tf": ("sbuf", [128, 3], "float32"),
    "ip": ("sbuf", [128, 1], "int32"),
    "ii": ("sbuf", [128, 3], "int32"),
    "cf": ("sbuf", [128, 4], "float32"),
    "pf": ("sbuf", [128, 1], "float32"),
    "icol": ("sbuf", [128, 128], "bfloat16"),
    "destc": ("sbuf", [128, 16], "float32"),
    "constK": ("sbuf", [128, 256], "bfloat16"),
    "cst4": ("sbuf", [128, 4], "float32"),
    "mx": ("sbuf", [128, 128], "bfloat16"),
    "my": ("sbuf", [128, 128], "bfloat16"),
    "mtri": ("sbuf", [128, 128], "bfloat16"),
    "a2": ("sbuf", [128, 128], "bfloat16"),
    "maskc": ("sbuf", [128, 8], "bfloat16"),
    "ctile": ("sbuf", [128, 80], "float32"),
    "dd": ("sbuf", [128, 16], "bfloat16"),
    "sc": ("sbuf", [128, 4], "float32"),
    "bd": ("sbuf", [128, 32], "bfloat16"),
    "aall": ("sbuf", [128, 256], "bfloat16"),
    "r1": ("sbuf", [128, 8], "bfloat16"),
    "r2": ("sbuf", [128, 8], "bfloat16"),
    "newx": ("sbuf", [128, 208], "bfloat16"),
    "tmpo": ("sbuf", [128, 8], "float32"),
    "soff": ("sbuf", [128, 12], "uint16"),
    "send": ("sbuf", [128, 16 * STR], "bfloat16"),
    "land": ("sbuf", [128, 12, LSTR], "bfloat16"),
    "tmp": ("sbuf", [128, 12, 2], "float32"),
    "roff": ("sbuf", [128, 24], "uint16"),
    "flat": ("sbuf", [128, 12 * CAP], "bfloat16"),
    "win": ("sbuf", [128, WIN], "bfloat16"),
    "pc": ("psum", [128, 512], "float32"),
    "pt": ("psum", [128, 512], "float32"),
}
SEMAPHORES = ["cv", "cs", "cp", "cg", "s_pos", "s_new", "s_tab1", "s_tab2", "s_y", "s_go", "s_c", "s_hn", "s_h", "s_z",
              "s_dir", "s_cross", "s_late", "loc"]


def _engines(mask):
    return [e for e in range(16) if (mask >> e) & 1]


def _mk(es):
    return sum(1 << e for e in es)


def _pow2(n):
    p = 1
    while p * 2 <= n:
        p *= 2
    return p


def _plan(cores, topo):
    classes = []
    for r, c in enumerate(cores):
        for cl in classes:
            a, b = topo.chip(cores[cl[0]]), topo.chip(c)
            if a == b or topo.same_plane(a, b):
                cl.append(r)
                break
        else:
            classes.append([r])
    order = [r for cl in classes for r in cl]
    xpos = {r: x for x, r in enumerate(order)}
    direct, relay, helper = {}, {}, {}
    for r, c in enumerate(cores):
        direct[r] = [d for d in range(len(cores)) if d != r and topo.may_write(c, cores[d])]
        far = [d for d in range(len(cores)) if d != r and not topo.may_write(c, cores[d])]
        relay[r] = []
        if not far:
            continue
        hs = [h for h in range(128) if topo.chip(h) == topo.chip(c) and h not in cores and topo.die(h) == topo.die(c)
              and all(topo.may_write(h, cores[d]) for d in far)]
        per = (len(far) + len(hs) - 1) // len(hs)
        rot = [cl for cl in classes if r in cl][0].index(r)
        for i, h in enumerate(hs):
            part = far[i * per:(i + 1) * per]
            if part:
                k = rot % len(part)
                part = part[k:] + part[:k]
                relay[r].append((h, part))
                helper[h] = (r, part)
    return classes, order, xpos, direct, relay, helper


def _hop2_calls(topo, h, part, cores):
    es = _engines(topo.mask(h, cores[part[0]]))
    calls, rest = [], list(part)
    while rest:
        m = min(_pow2(len(rest)), len(es))
        per = len(es) // m
        calls.append([(d, es[q * per:(q + 1) * per]) for q, d in enumerate(rest[:m])])
        rest = rest[m:]
    return calls


def _xfer(T, topo, dst_core, es, sem, src, dst):
    rid, pid, _ = topo.addr(dst_core)
    return RemoteDMATransfer(dst_ids=[DstId(rid=rid, pnc=pid)], dma_engine_mask=_mk(es), remote_sem=sem, src=src, dst=dst)


def rank_program(g, core, T, topo):
    cores = list(T.cores)
    classes, order, xpos, direct, relay, helper = _plan(cores, topo)
    rank = T.rank_of(core)
    if rank is None and core not in helper:
        return

    Op, Act = AluOpType, ActivationFunctionType
    V, S, PE, Y = g.vector, g.scalar, g.tensor, g.sync
    eng = {"v": V, "s": S, "p": PE, "g": g, "y": Y}
    sname = {"v": "cv", "s": "cs", "p": "cp", "g": "cg"}
    cnt = {"v": 0, "s": 0, "p": 0, "g": 0}
    seen = {k: {} for k in eng}
    USED = len(cores) * STR

    def pre(q, *deps):
        deps = list(deps)
        if q in cnt:
            deps.append((sname[q], cnt[q]))
        for name, val in deps:
            if seen[q].get(name, 0) < val:
                eng[q].wait_ge(T.sem[name], val)
                seen[q][name] = val

    def op(q, ins):
        cnt[q] += 1
        ins.then_inc(T.sem[sname[q]], 1)
        return (sname[q], cnt[q])

    def arrivals(r):
        mine = [cl for cl in classes if r in cl][0]
        first, later = [], []
        for s in order:
            for h, part in relay[s]:
                for ci, call in enumerate(_hop2_calls(topo, h, part, cores)):
                    for d, es in call:
                        if d == r:
                            (first if ci == 0 else later).append((s, len(es)))
        return mine, first, later

    def lslot(r, s):
        mine, first, later = arrivals(r)
        return (list(mine) + [t for t, _ in first] + [t for t, _ in later]).index(s)

    def hop1_engines(r):
        out = []
        for i, (h, _) in enumerate(relay[r]):
            es = _engines(topo.mask(cores[r], h))
            per = _pow2(len(es) // len(relay[r]))
            out.append(es[len(es) - (i + 1) * per:len(es) - i * per])
        return out

    def fill_buckets(*deps):
        pre("v", *deps); op("v", V.tensor_tensor(T.tmpo[:], T.newx[:, 192:200], T.newx[:, 200:208], Op.add))
        pre("v"); op("v", V.tensor_scalar(T.soff[:, 0:8], T.tmpo[:], -128.0, None, Op.add))
        pre("v")
        return op("v", V.tensor_copy(T.send[:, 0:16 * STR].indirect(T.soff[:, 0:12]), T.newx[:, 0:192]))

    if rank is None:
        src, part = helper[core]
        hs = [h for h, _ in relay[src]]
        i, n = hs.index(core), len(hs)
        heng = len(hop1_engines(src)[i])
        e_far = _engines(topo.mask(core, cores[part[0]]))
        pre("v"); d_zero = op("v", V.memset(T.send[:, 0:USED], 0.0))
        pre("g", d_zero)
        rid, pid, _ = topo.addr(cores[src])
        a, b = USED * i // n, USED * (i + 1) // n
        g.remote_dma(T.send[:, a:b], T.send[:, a:b], T.sem.s_z, T.sem.loc, pid, rid, _mk(e_far))
        d_send = fill_buckets(("s_c", heng), ("s_hn", heng), ("s_h", heng), ("loc", len(e_far)))
        pre("g", d_send)
        tot = len(e_far)
        for ci, call in enumerate(_hop2_calls(topo, core, part, cores)):
            sem = T.sem.s_cross if ci == 0 else T.sem.s_late
            g.remote_dma_fused([_xfer(T, topo, cores[d], es, sem, T.send[:, STR * d:STR * d + MSG],
                                      T.land[:, lslot(d, src), 0:MSG]) for d, es in call], local_sem=T.sem.loc)
            tot += sum(len(es) for _, es in call)
        g.wait_ge(T.sem.loc, tot)
        return

    xs = xpos[rank]
    mine, first, later = arrivals(rank)
    off_chip = [d for d in direct[rank] if topo.chip(cores[d]) != topo.chip(core)]
    on_chip = [d for d in direct[rank] if topo.chip(cores[d]) == topo.chip(core)]
    e_off = _engines(topo.mask(core, cores[off_chip[0]])) if off_chip else []
    loc = 0

    def to_helpers(ap, sem):
        trs = [_xfer(T, topo, h, es, sem, ap, ap) for (h, _), es in zip(relay[rank], hop1_engines(rank))]
        if trs:
            g.remote_dma_fused(trs, local_sem=T.sem.loc)
        return sum(len(es) for es in hop1_engines(rank))

    Y.dma_start(T.posP[:], T.pos[:]).then_inc(T.sem.s_pos, 16)
    Y.dma_start(T.newx[:, 0:128], T.new[:]).then_inc(T.sem.s_new, 16)
    Y.dma_start(T.win[:, 0:H1], T.tab[:, 0:H1]).then_inc(T.sem.s_tab1, 16)

    pre("g"); d_ip = op("g", g.iota(T.ip[:], [[0, 1]], 0, 1))
    pre("g"); d_cst4 = op("g", g.iota(T.cst4[:], [[1, 2], [2, 2]], CAP, 0, allow_small_or_imprecise_dtypes=True))
    pre("g"); d_icol = op("g", g.iota(T.icol[:], [[1, 128]], 0, 0, allow_small_or_imprecise_dtypes=True))
    pre("g"); d_dest = op("g", g.iota(T.destc[:], [[1, 16]], 0, 0, allow_small_or_imprecise_dtypes=True))
    pre("v", d_ip); op("v", V.tensor_scalar(T.ii[:, 2:3], T.ip[:], 15, None, Op.bitwise_and))
    pre("v"); op("v", V.tensor_scalar(T.cf[:, 2:3], T.ii[:, 2:3], float(STR), None, Op.mult))
    pre("v", d_cst4); d_soffc = op("v", V.tensor_scalar(T.soff[:, 8:12], T.cst4[:], T.cf[:, 2:3], None, Op.add))
    pre("g", d_soffc)
    loc += to_helpers(T.soff[:, 8:12], T.sem.s_c)
    pre("g"); d_constK = op("g", g.iota(T.constK[:], [[16, 2], [0, 8], [1, 16]], 128, 0, allow_small_or_imprecise_dtypes=True))
    pre("g", ("s_new", 16))
    loc += to_helpers(T.newx[:, 0:128], T.sem.s_hn)

    pre("v"); op("v", V.tensor_copy(T.pf[:], T.ip[:]))
    pre("v"); d_cf3 = op("v", V.tensor_scalar(T.cf[:, 3:4], T.ii[:, 2:3], -64.0, None, Op.add))
    pre("v"); op("v", V.tensor_scalar(T.ii[:, 0:1], T.ip[:], 3, None, Op.logical_shift_right))
    pre("v"); op("v", V.tensor_scalar(T.ii[:, 1:2], T.ip[:], 7, None, Op.bitwise_and))
    pre("v"); op("v", V.tensor_scalar(T.cf[:, 0:1], T.ii[:, 0:1], 128.0, None, Op.add))
    pre("v"); op("v", V.tensor_copy(T.cf[:, 1:2], T.ii[:, 1:2]))
    pre("v", d_icol); op("v", V.tensor_scalar(T.mx[:], T.icol[:], T.pf[:, 0:1], None, Op.is_gt))
    pre("v"); op("v", V.tensor_scalar(T.my[:], T.icol[:], T.pf[:, 0:1], 128.0, Op.is_equal, Op.mult))
    pre("v"); op("v", V.tensor_tensor(T.mtri[:], T.mx[:], T.my[:], Op.add))
    pre("v"); op("v", V.tensor_scalar(T.maskc[:], T.icol[:, 0:8], T.cf[:, 1:2], None, Op.is_equal))
    pre("v", d_constK); op("v", V.tensor_scalar(T.a2[:], T.constK[:, 0:128], T.cf[:, 0:1], None, Op.is_equal))

    pre("s", d_cf3, d_icol)
    op("s", S.activation(T.ctile[:, 0:64], T.icol[:, 0:64], Act.Identity, bias=T.cf[:, 3:4], scale=0.0))
    for h in range(2):
        pre("s"); op("s", S.activation(T.ctile[:, 32 * h:32 * h + 16], T.icol[:, 0:16], Act.Identity,
                                       bias=float(COLS + 64 * (2 * xs + h) - 8192), scale=0.0))
    pre("s"); d_ctile = op("s", S.activation(T.ctile[:, 64:80], T.icol[:, 0:16], Act.Identity, bias=10000.0, scale=0.0))

    pre("v", ("s_pos", 16)); op("v", V.tensor_scalar(T.ti[:, 0:1], T.posP[:], 12, None, Op.logical_shift_right))
    pre("v"); d_df = op("v", V.tensor_copy(T.tf[:, 0:1], T.ti[:, 0:1]))
    pre("v", d_dest); d_dd = op("v", V.tensor_scalar(T.dd[:], T.destc[:], T.tf[:, 0:1], None, Op.is_equal))
    pre("p", d_dd); d_pc = op("p", PE.matmul(T.pc[:, 0:16], T.mtri[:], T.dd[:], True, True))
    pre("s", d_df); op("s", S.activation(T.sc[:, 2:3], T.tf[:, 0:1], Act.Identity, scale=float(STR)))
    pre("s"); d_r1 = op("s", S.activation(T.r1[:], T.maskc[:], Act.Identity, scale=T.sc[:, 2:3]))
    pre("p", d_r1); op("p", PE.matmul(T.pt[:, 64:72], T.a2[:], T.r1[:], True, True))
    pre("v"); op("v", V.tensor_scalar(T.ti[:, 1:2], T.posP[:], 4032, None, Op.bitwise_and))
    pre("v"); op("v", V.tensor_scalar(T.ti[:, 2:3], T.posP[:], 63, None, Op.bitwise_and))
    pre("v"); d_tf = op("v", V.tensor_copy(T.tf[:, 1:3], T.ti[:, 1:3]))
    pre("s", d_tf); op("s", S.activation(T.sc[:, 0:1], T.tf[:, 1:2], Act.Identity, bias=-8192.0))
    pre("s"); op("s", S.activation(T.sc[:, 1:2], T.tf[:, 2:3], Act.Identity, bias=-128.0))
    pre("s"); op("s", S.activation(T.bd[:, 0:16], T.dd[:], Act.Identity, scale=T.sc[:, 0:1]))
    pre("s"); d_bd = op("s", S.activation(T.bd[:, 16:32], T.dd[:], Act.Identity, scale=T.sc[:, 1:2]))
    pre("v", d_pc); d_kb = op("v", V.tensor_reduce(T.sc[:, 3:4], T.pc[:, 0:16], AxisListType.X, Op.max))
    pre("s", d_kb); d_r2 = op("s", S.activation(T.r2[:], T.maskc[:], Act.Identity, scale=T.sc[:, 3:4]))
    pre("v"); d_aall = op("v", V.tensor_scalar(T.aall[:], T.constK[:], T.sc[:, 3:4], None, Op.is_equal))
    pre("p", d_aall, d_bd); op("p", PE.matmul(T.pt[:, 0:32], T.aall[:, 0:128], T.bd[:], True, True))
    pre("p"); op("p", PE.matmul(T.pt[:, 32:64], T.aall[:, 128:256], T.bd[:], True, True))
    pre("p", d_r2); d_pt = op("p", PE.matmul(T.pt[:, 72:80], T.a2[:], T.r2[:], True, True))
    pre("v", d_pt, d_ctile); d_msg = op("v", V.tensor_tensor(T.newx[:, 128:208], T.pt[:, 0:80], T.ctile[:], Op.min))

    pre("g", d_msg)
    loc += to_helpers(T.newx[:, 128:208], T.sem.s_h)
    n_z = sum(len(_engines(topo.mask(h, cores[part[0]]))) for h, part in relay[rank])
    if not relay[rank]:
        pre("v"); op("v", V.memset(T.send[:, 0:USED], 0.0))
    d_send = fill_buckets(("s_new", 16), ("s_z", n_z))
    pre("g", d_send)
    trs, n_dir = [], 0
    per = _pow2(len(e_off) // len(off_chip)) if off_chip else 0
    for i, d in enumerate(off_chip):
        trs.append(_xfer(T, topo, cores[d], e_off[i * per:(i + 1) * per], T.sem.s_dir,
                         T.send[:, STR * d:STR * d + MSG], T.land[:, lslot(d, rank), 0:MSG]))
        n_dir += per
    for d in on_chip:
        es = [e for e in _engines(topo.mask(core, cores[d])) if e not in e_off]
        es = es[:_pow2(len(es) // len(on_chip))]
        trs.append(_xfer(T, topo, cores[d], es, T.sem.s_dir,
                         T.send[:, STR * d:STR * d + MSG], T.land[:, lslot(d, rank), 0:MSG]))
        n_dir += len(es)
    g.remote_dma_fused(trs, local_sem=T.sem.loc)
    g.sem_inc(T.sem.s_go, 1)
    loc += n_dir

    pre("y", ("s_go", 1))
    Y.dma_start(T.win[:, H1:COLS], T.tab[:, H1:COLS]).then_inc(T.sem.s_tab2, 16)

    pre("v")
    d_own = op("v", V.tensor_copy(T.land[:, lslot(rank, rank), 0:MSG], T.send[:, STR * rank:STR * rank + MSG]))

    def batch(a, b, deps, late):
        pre("s", *deps)
        d_flat = op("s", S.activation(T.flat[:, CAP * a:CAP * b], T.land[:, a:b, 0:CAP], Act.Copy))
        pre("v", *deps)
        op("v", V.tensor_tensor(T.tmp[:, a:b, :], T.land[:, a:b, CAP:CAP + 2], T.land[:, a:b, CAP + 2:CAP + 4], Op.add))
        pre("v"); op("v", V.tensor_scalar(T.roff[:, 2 * a:2 * b], T.tmp[:, a:b, :], 8320.0, None, Op.add))
        pre("v", d_flat, *late)
        return op("v", V.tensor_copy(T.win[:, 0:WIN].indirect(T.roff[:, 2 * a:2 * b]), T.flat[:, CAP * a:CAP * b]))

    n0, n1, n2 = len(mine), len(first), len(later)
    d_last = batch(0, n0, [d_own, ("s_dir", n_dir)], [("s_tab1", 16), ("s_tab2", 16)])
    if n1:
        d_last = batch(n0, n0 + n1, [("s_cross", sum(e for _, e in first))], [])
    if n2:
        d_last = batch(n0 + n1, n0 + n1 + n2, [("s_late", sum(e for _, e in later))], [])

    pre("y", d_last)
    Y.dma_start(T.y[:], T.win[:, 0:COLS]).then_inc(T.sem.s_y, 16)
    Y.wait_ge(T.sem.s_y, 16)

    g.wait_ge(T.sem.loc, loc)
    pre("g", ("cv", cnt["v"]), ("cs", cnt["s"]), ("cp", cnt["p"]))
